import numpy as np
import ml_dtypes


def mxq(x, axis, fmt="e4m3"):
    dtype, down = {"e4m3": (ml_dtypes.float8_e4m3fn, 7), "e5m2": (ml_dtypes.float8_e5m2, 14)}[fmt]
    v = np.moveaxis(np.asarray(x, np.float32).astype(ml_dtypes.bfloat16).astype(np.float64), axis, -1)
    blocks = v.reshape(v.shape[:-1] + (-1, 32))
    amax = np.abs(blocks).max(-1, keepdims=True)
    byte = np.maximum(np.where(amax > 0, np.frexp(amax)[1] - 1 + 127, 0) - down, 1)
    scale = np.exp2(byte - 127.0)
    codes = (blocks / scale).astype(np.float32).astype(dtype).astype(np.float64)
    return np.moveaxis((codes * scale).reshape(v.shape), -1, axis)


WIDE = False


def mx_kscale(k):
    if not WIDE:
        return np.ones(k)
    levels = np.array([10, -10, 5, -5, 0])
    if k % 512:
        return np.exp2(np.random.permutation(np.resize(levels, k // 32))).repeat(32)
    a = np.empty((k // 512, 16))
    for p in range(k // 512):
        a[p, :8] = np.random.permutation(np.resize(levels, 8))
        for g in range(8):
            far = levels[np.abs(levels - a[p, g]) >= 10]
            a[p, g + 8] = far[np.random.randint(len(far))]
    return np.exp2(a.ravel()).repeat(32)


BF16 = ml_dtypes.bfloat16


def bf(x):
    return np.asarray(x, np.float32).astype(BF16)


def f64(x):
    return np.asarray(x).astype(np.float64)


E2M1 = np.array([0.0, 0.5, 1.0, 1.5, 2.0, 3.0, 4.0, 6.0, -0.0, -0.5, -1.0, -1.5, -2.0, -3.0, -4.0, -6.0])


def pack_weight(w, fmt):
    k, n = w.shape
    w = f64(bf(w)).reshape(k // 32, 32, n)
    amax = np.abs(w).max(1)
    if fmt == "e4m3":
        byte = np.frexp(amax)[1] - 1 + 127 - 7
    else:
        mant, ex = np.frexp(amax / 6.0)
        byte = np.where(mant > 0.5, ex, ex - 1) + 127
    byte = np.clip(np.where(amax > 0, byte, 1), 1, 254)
    scaled = (w * np.exp2(127.0 - byte)[:, None, :]).reshape(k, n).astype(np.float32)
    by_word = np.ascontiguousarray(scaled.reshape(k // 512, 128, 4, n).transpose(0, 1, 3, 2))
    if fmt == "e4m3":
        words = by_word.astype(ml_dtypes.float8_e4m3fn).view(np.uint8)
    else:
        c = by_word.astype(ml_dtypes.float4_e2m1fn).view(np.uint8) & 0xF
        words = c[..., 0::2] | (c[..., 1::2] << 4)
    return np.ascontiguousarray(words), np.ascontiguousarray(byte.astype(np.uint8).reshape(k // 512, 16, n))


def unpack_weight(words, scales, fmt):
    g, p, n, _ = words.shape
    if fmt == "e4m3":
        vals = np.ascontiguousarray(words).view(ml_dtypes.float8_e4m3fn).astype(np.float64)
    else:
        nib = np.empty((g, p, n, 4), np.uint8)
        nib[..., 0::2] = words & 0xF
        nib[..., 1::2] = words >> 4
        vals = E2M1[nib]
    vals = vals * np.repeat(np.exp2(scales.astype(np.float64) - 127.0), 8, axis=1)[..., None]
    return vals.transpose(0, 1, 3, 2).reshape(g * 512, n)
def pack4(w):
    words, scales = pack_weight(w, "e2m1")
    return words.reshape(words.shape[0], 128, -1), scales


def unpack4(words, scales):
    return unpack_weight(words.reshape(words.shape[0], 128, -1, 2), scales, "e2m1")


F, D, M, P, R = 1024, 1536, 1024, 2048, 512


def draw0():
    s, t, u = mx_kscale(D), mx_kscale(M), mx_kscale(F)
    sigma = bf(np.random.uniform(0.4, 1.6, M))
    lam = bf(np.random.uniform(0.2, 1.0, F))
    meas = bf(np.random.standard_normal((F, D)) * s * u[:, None])
    us = bf(np.random.standard_normal((D, M)) / np.sqrt(D) * f64(sigma) / s[:, None] * t)
    vt_words, vt_scales = pack4(np.random.standard_normal((M, P)) / np.sqrt(M) / t[:, None])
    basis = bf(np.random.standard_normal((R, F)) / np.sqrt(F) / u)
    return {"meas": meas, "us": us, "sigma": sigma, "lam": lam,
            "vt_words": vt_words, "vt_scales": vt_scales, "basis": basis}


def core(meas, us, sigma, lam, vt_words, vt_scales, basis):
    c = mxq(f64(meas), 1, "e4m3") @ mxq(f64(us), 0, "e4m3")
    h = c / (f64(sigma)[None, :] ** 2 + f64(lam)[:, None])
    image = mxq(h, 1, "e4m3") @ unpack4(vt_words, vt_scales)
    comps = mxq(f64(basis), 1, "e4m3") @ mxq(h, 0, "e4m3")
    return image, comps


def e4m3fn_bytes(y):
    return np.clip(np.asarray(y, np.float64), -448.0, 448.0).astype(np.float32).astype(ml_dtypes.float8_e4m3fn).view(np.uint8)


def e4m3fn_values(b):
    return np.asarray(b, np.uint8).view(ml_dtypes.float8_e4m3fn).astype(np.float64)


def setup_inputs():
    d = draw0()
    x0 = np.asarray(d['basis']).astype(np.float64)
    s = (np.max(np.abs(x0), axis=(0,), keepdims=True) / 448.0).astype(np.float32)
    out = {}
    for k, v in d.items():
        if k == 'basis':
            out['basis_bytes'] = e4m3fn_bytes(x0 / s.astype(np.float64))
            out['basis_scale'] = s
        else:
            out[k] = v
    return out


def reference(meas, us, sigma, lam, vt_words, vt_scales, basis_bytes, basis_scale):
    return core(meas, us, sigma, lam, vt_words, vt_scales, e4m3fn_values(basis_bytes) * basis_scale.astype(np.float64))

@@ -1,0 +1,378 @@
+from contextlib import ExitStack
+
+import concourse.mybir as mybir
+from concourse.masks import make_identity
+
+F, D, M, P, R = 1024, 1536, 1024, 2048, 512
+FLOPS = 2 * (F * D * M + F * M * P + R * F * M)
+
+F32 = mybir.dt.float32
+BF16 = mybir.dt.bfloat16
+U32 = mybir.dt.uint32
+U8 = mybir.dt.uint8
+I32 = mybir.dt.int32
+E4M3 = mybir.dt.float8_e4m3fn
+FP8X4 = mybir.dt.float8_e4m3fn_x4
+FP4X4 = mybir.dt.float4_e2m1fn_x4
+ACT = mybir.ActivationFunctionType
+MULT = mybir.AluOpType.mult
+SUB = mybir.AluOpType.subtract
+
+PD = D // 512
+PM = M // 512
+PF = F // 512
+AB, TP = 5, 3
+
+
+def tile_spectral_tikhonov_imaging_s8_kernel(
+    tc, meas, us, sigma, lam, vt_words, vt_scales, basis_bytes, basis_scale, image, comps
+):
+    nc = tc.nc
+    with ExitStack() as ctx:
+        keep = ctx.enter_context(tc.tile_pool(name="keep", bufs=1))
+        work = ctx.enter_context(tc.tile_pool(name="work", bufs=2))
+        stage = ctx.enter_context(tc.tile_pool(name="stage", bufs=6))
+        psum = ctx.enter_context(tc.psum_pool(name="psum", bufs=1))
+
+        ctx.enter_context(tc.manual_schedule())
+
+        lam_raw = keep.tile([128, F], BF16, name="lam_raw")
+        nc.vector.memset(lam_raw[0:64, :], 0.0)
+        d_rhs = keep.tile([128, F], BF16, name="d_rhs")
+        nc.gpsimd.memset(d_rhs[:], 1.0)
+        d_cols = keep.tile([128, PM * 4, 128], BF16, name="d_cols")
+        nc.vector.memset(d_cols[:], 0.0)
+        nc.vector.memset(d_cols[:, :, 0:33:32], 1.0)
+        warm = keep.tile([128, 1], F32, name="warm")
+        nc.vector.memset(warm[:], 1.0)
+        nc.scalar.activation(out=warm[:], in_=warm[:], func=ACT.Abs_reciprocal_sqrt)
+        ident = keep.tile([128, 128], F32, name="ident")
+        make_identity(nc, ident[:])
+        ident_b = keep.tile([128, 128], BF16, name="ident_b")
+        make_identity(nc, ident_b[:])
+        vs = keep.tile([128, PM, P], U8, name="vs", align_bytes=64)
+        nc.gpsimd.memset(vs[:].bitcast(I32), 0)
+
+        sig = keep.tile([128, PM * 4], BF16, name="sig")
+        nc.sync.dma_start(out=sig[:].rearrange("q (j t) -> q j t", j=PM), in_=sigma.rearrange("(j q t) -> q j t", j=PM, q=128))
+        nc.sync.dma_start(out=lam_raw[0:64:32, :], in_=lam.partition_broadcast(2))
+        nc.sync.dma_start(out=d_rhs[64:66, :], in_=lam.partition_broadcast(2))
+
+        raw_meas = []
+        for pr in range(4):
+            raw_meas.append(keep.tile([128, 2, D], BF16, name="raw_meas%d" % pr))
+        meas_v = meas.rearrange("(g p t) d -> g p t d", g=2, p=128)
+        us_v = us.rearrange("(g p k) m -> g p k m", p=128, k=4)
+        raw_us = {}
+
+        def load_meas(pr):
+            nc.sync.dma_start(out=raw_meas[pr][:], in_=meas_v[pr // 2, :, 2 * (pr % 2) : 2 * (pr % 2) + 2, :])
+
+        load_meas(0)
+        for j in range(PM):
+            if j == 1:
+                load_meas(1)
+            for g in range(PD):
+                t = stage.tile([128, 4, 512], BF16, name="raw_us", tag="stage", bufs=6)
+                nc.sync.dma_start(out=t[:], in_=us_v[g, :, :, 512 * j : 512 * j + 512])
+                raw_us[j, g] = t
+        for q in range(4):
+            nc.sync.dma_start(
+                out=vs[32 * q : 32 * q + 4, :, :].bitcast(I32),
+                in_=vt_scales[:, 4 * q : 4 * q + 4, :].rearrange("g r n -> r g n").bitcast(I32),
+            )
+        vt = keep.tile([128, PM, 2 * P], U8, name="vt", align_bytes=64)
+        nc.sync.dma_start(out=vt[:], in_=vt_words.rearrange("g p n -> p g n"))
+        for pr in range(2, 4):
+            load_meas(pr)
+        b_raw = keep.tile([128, 4, F], U8, name="b_raw")
+        nc.sync.dma_start(out=b_raw[:], in_=basis_bytes.rearrange("(r p) f -> p r f", p=128))
+        b_scale = keep.tile([128, F], F32, name="b_scale")
+        nc.sync.dma_start(out=b_scale[:], in_=basis_scale.rearrange("o k -> (o k)").partition_broadcast(128))
+
+        s2 = keep.tile([128, PM * 4], F32, name="s2")
+        nc.vector.tensor_tensor(out=s2[:], in0=sig[:], in1=sig[:], op=MULT)
+        nc.vector.tensor_tensor(out=d_rhs[0:64, :], in0=lam_raw[0:64, :], in1=lam_raw[0:64, :], op=MULT)
+        lam_sq = keep.tile([128, F], F32, name="lam_sq")
+        nc.scalar.activation(out=lam_sq[0:64, :], in_=lam_raw[0:64, :], func=ACT.Square)
+        nc.vector.tensor_scalar(out=d_cols[:, :, 64], in0=s2[:], scalar1=2.0, scalar2=None, op0=MULT)
+        s4 = keep.tile([128, PM * 4], F32, name="s4")
+        nc.vector.tensor_tensor(out=s4[:], in0=s2[:], in1=s2[:], op=MULT)
+        nc.vector.scalar_tensor_tensor(out=d_cols[:, :, 65], in0=s2[:], scalar=2.0, in1=d_cols[:, :, 64], op0=MULT, op1=SUB)
+        nc.vector.tensor_copy(out=d_cols[:, :, 96], in_=s4[:])
+        rest = keep.tile([128, PM * 4], F32, name="rest")
+        nc.vector.tensor_tensor(out=rest[:], in0=s4[:], in1=d_cols[:, :, 96], op=SUB)
+        nc.vector.tensor_copy(out=d_cols[:, :, 97], in_=rest[:])
+        nc.vector.tensor_tensor(out=d_cols[:, :, 98], in0=rest[:], in1=d_cols[:, :, 97], op=SUB)
+        nc.vector.tensor_tensor(out=d_rhs[32:64, :], in0=lam_sq[32:64, :], in1=d_rhs[32:64, :], op=SUB)
+        d_lhs = keep.tile([128, PM * 4, 128], BF16, name="d_lhs")
+
+        def square_lhs():
+            d_turn = psum.tile([128, PM * 4, 128], BF16, name="d_turn", tag="acc", bufs=AB)
+            for i in range(PM * 4):
+                nc.tensor.transpose(d_turn[:, i, :], d_cols[:, i, :], ident_b[:])
+            nc.vector.tensor_copy(out=d_lhs[:], in_=d_turn[:])
+
+        copy_on = {"S": nc.scalar.copy, "V": nc.vector.tensor_copy}
+        r2, tiles = {}, {}
+
+        def weights(c, j):
+            bank = psum.tile([128, 4, 128], F32, name="wb", tag="tp", bufs=TP)
+            for t in range(4):
+                nc.tensor.matmul(
+                    out=bank[:, t, :],
+                    lhsT=d_lhs[:, 4 * j + t, :],
+                    rhs=d_rhs[:, 512 * (c // 4) + c % 4 : 512 * (c // 4) + 512 : 4],
+                    start=True,
+                    stop=True,
+                )
+            r2[c, j] = work.tile([128, 128, 4], F32, name="r2", bufs=16)
+            nc.scalar.activation(out=r2[c, j][:], in_=bank[:].rearrange("q t f -> q f t"), func=ACT.Abs_reciprocal_sqrt)
+
+        def turn_meas(pr, g, eng):
+            if g == 0:
+                tiles["mc", pr] = keep.tile([128, PD, 256], U32, name="mc%d" % pr, align_bytes=64)
+                tiles["ms", pr] = keep.tile([128, PD, 256], U8, name="ms%d" % pr, align_bytes=64)
+            words = raw_meas[pr][:].bitcast(F32)
+            tp = psum.tile([128, 2, 2, 128], F32, name="tp", tag="tp", bufs=TP)
+            for c in range(2):
+                for u in range(2):
+                    nc.tensor.transpose(tp[:, c, u, :], words[:, c, 256 * g + u : 256 * g + 256 : 2], ident[:])
+            grouped = work.tile([128, 1024], BF16, name="mg", align_bytes=64, bufs=4)
+            tiles["mg", pr, g] = grouped
+            dst = grouped[:].bitcast(F32).rearrange("p (c r u) -> p c r u", c=2, u=2)
+            copy_on[eng](out=dst, in_=tp[:].rearrange("p c u r -> p c r u"))
+
+        def quantize_meas(pr, g):
+            nc.vector.quantize_mx(
+                out=tiles["mc", pr][:, g, :].bitcast(FP8X4), scales=tiles["ms", pr][:, g, :], in_=tiles["mg", pr, g][:]
+            )
+
+        uc = keep.tile([128, PD, M], U32, name="uc", align_bytes=64)
+        usc = keep.tile([128, PD, M], U8, name="usc", align_bytes=64)
+
+        def group_us(j, g, eng):
+            grouped = work.tile([128, 4, 128, 4], BF16, name="ug", align_bytes=64, bufs=3)
+            tiles["ug", j, g] = grouped
+            copy_on[eng](out=grouped[:], in_=raw_us[j, g][:].rearrange("p k (q t) -> p t q k", t=4))
+
+        def quantize_us(j, g):
+            nc.vector.quantize_mx(
+                out=uc[:, g, 512 * j : 512 * j + 512].bitcast(FP8X4),
+                scales=usc[:, g, 512 * j : 512 * j + 512],
+                in_=tiles["ug", j, g][:].rearrange("p t q k -> p (t q k)"),
+            )
+
+        hb, hc, hs = {}, {}, {}
+
+        def project(c, j):
+            bank = psum.tile([128, 4, 128], F32, name="cb", tag="acc", bufs=AB)
+            pr, half = c // 2, c % 2
+            mc, ms = tiles["mc", pr], tiles["ms", pr]
+            for t in range(4):
+                col = 512 * j + 128 * t
+                for g in range(PD):
+                    nc.tensor.matmul_mx(
+                        out=bank[:, t, :],
+                        lhsT=uc[:, g, col : col + 128].bitcast(FP8X4),
+                        lhsT_scale=usc[:, g, col : col + 128],
+                        rhs=mc[:, g, 128 * half : 128 * half + 128].bitcast(FP8X4),
+                        rhs_scale=ms[:, g, 128 * half : 128 * half + 128],
+                        start=(g == 0),
+                        stop=(g == PD - 1),
+                    )
+            tiles["cb", c, j] = bank
+
+        def weigh(c, j):
+            if j == 0:
+                hb[c] = work.tile([128, PM, 128, 4], BF16, name="hb", align_bytes=64, bufs=6)
+            bank = tiles["cb", c, j]
+            nc.vector.tensor_tensor(out=hb[c][:, j], in0=bank[:].rearrange("q t f -> q f t"), in1=r2[c, j][:], op=MULT)
+
+        def quantize_chunk(c):
+            hc[c] = work.tile([128, PM, 128], U32, name="hc", align_bytes=64, bufs=3)
+            hs[c] = work.tile([128, PM, 128], U8, name="hs", align_bytes=64, bufs=3)
+            nc.vector.quantize_mx(
+                out=hc[c][:].rearrange("q j f -> q (j f)").bitcast(FP8X4),
+                scales=hs[c][:].rearrange("q j f -> q (j f)"),
+                in_=hb[c][:].rearrange("q j f t -> q (j f t)"),
+            )
+
+        image_v = image.rearrange("(g p t) n -> g t p n", g=2, p=128)
+
+        def image_part(c, n, eng):
+            if n % 2 == 0:
+                tiles["ob"] = stage.tile([128, 1024], F32, name="ob", tag="stage", bufs=6)
+            ob = tiles["ob"]
+            bank = psum.tile([128, 512], F32, name="ib", tag="acc", bufs=AB)
+            for j in range(PM):
+                nc.tensor.matmul_mx(
+                    out=bank[:],
+                    lhsT=hc[c][:, j, :].bitcast(FP8X4),
+                    lhsT_scale=hs[c][:, j, :],
+                    rhs=vt[:, j, 1024 * n : 1024 * n + 1024].bitcast(FP4X4),
+                    rhs_scale=vs[:, j, 512 * n : 512 * n + 512],
+                    start=(j == 0),
+                    stop=(j == PM - 1),
+                )
+            copy_on[eng](out=ob[:, 512 * (n % 2) : 512 * (n % 2) + 512], in_=bank[:])
+            if n % 2 == 1:
+                two = slice(512 * n - 512, 512 * n + 512)
+                nc.sync.dma_start(out=image_v[c // 4, c % 4, :, two], in_=ob[:])
+
+        bc = keep.tile([128, PF, R], U32, name="bc", align_bytes=64)
+        bsc = keep.tile([128, PF, R], U8, name="bsc", align_bytes=64)
+
+        def widen_basis(r):
+            tiles["bw", r] = keep.tile([128, F], BF16, name="bw%d" % r)
+            nc.vector.tensor_tensor(out=tiles["bw", r][:], in0=b_raw[:, r, :].bitcast(E4M3), in1=b_scale[:], op=MULT)
+
+        def turn_basis(g, h, eng):
+            if h == 0:
+                tiles["bg", g] = work.tile([128, 2, 1024], BF16, name="bg", align_bytes=64)
+            tp = psum.tile([128, 2, 2, 128], F32, name="tp", tag="tp", bufs=TP)
+            for r in range(2):
+                words = tiles["bw", 2 * h + r][:].bitcast(F32)
+                for u in range(2):
+                    nc.tensor.transpose(tp[:, r, u, :], words[:, 256 * g + u : 256 * g + 256 : 2], ident[:])
+            dst = tiles["bg", g][:, h].bitcast(F32).rearrange("p (r n u) -> p r n u", r=2, u=2)
+            copy_on[eng](out=dst, in_=tp[:].rearrange("p r u n -> p r n u"))
+
+        def quantize_basis(g):
+            nc.vector.quantize_mx(
+                out=bc[:, g, :].bitcast(FP8X4), scales=bsc[:, g, :], in_=tiles["bg", g][:].rearrange("p h n -> p (h n)")
+            )
+
+        ac, asc = {}, {}
+
+        def turn_group(g, j, u, eng):
+            if u == 0:
+                if j == 0:
+                    ac[g] = keep.tile([128, PM, 512], U32, name="ac%d" % g, align_bytes=64)
+                    asc[g] = keep.tile([128, PM, 512], U8, name="asc%d" % g, align_bytes=64)
+                tiles["ha"] = work.tile([128, 2, 256, 4], BF16, name="ha", align_bytes=64)
+            tp = psum.tile([128, 4, 128], F32, name="tp", tag="tp", bufs=TP)
+            for t in range(4):
+                words = hb[4 * g + t][:, j].rearrange("q f t -> q (f t)").bitcast(F32)
+                nc.tensor.transpose(tp[:, t, :], words[:, u:256:2], ident[:])
+            copy_on[eng](out=tiles["ha"][:, u], in_=tp[:].bitcast(BF16).rearrange("p t n -> p n t"))
+            tiles["ha", g, j] = tiles["ha"]
+
+        def quantize_group(g, j):
+            nc.vector.quantize_mx(
+                out=ac[g][:, j, :].bitcast(FP8X4), scales=asc[g][:, j, :], in_=tiles["ha", g, j][:].rearrange("p u n t -> p (u n t)")
+            )
+
+        def comps_part(r, j, eng):
+            if j == 0:
+                tiles["co"] = stage.tile([128, M], F32, name="co", tag="stage", bufs=6)
+            co = tiles["co"]
+            bank = psum.tile([128, 512], F32, name="ib", tag="acc", bufs=AB)
+            for g in range(PF):
+                nc.tensor.matmul_mx(
+                    out=bank[:],
+                    lhsT=bc[:, g, 128 * r : 128 * r + 128].bitcast(FP8X4),
+                    lhsT_scale=bsc[:, g, 128 * r : 128 * r + 128],
+                    rhs=ac[g][:, j, :].bitcast(FP8X4),
+                    rhs_scale=asc[g][:, j, :],
+                    start=(g == 0),
+                    stop=(g == PF - 1),
+                )
+            cols = slice(512 * j, 512 * j + 512)
+            copy_on[eng](
+                out=co[:, cols].rearrange("p (q u e) -> p q u e", u=2, e=2), in_=bank[:].rearrange("p (u q e) -> p q u e", u=2, e=2)
+            )
+            nc.sync.dma_start(out=comps[128 * r : 128 * r + 128, cols], in_=co[:, cols])
+
+        square_lhs()
+        for g in range(PD):
+            turn_meas(0, g, "S")
+        group_us(0, 0, "V")
+        group_us(0, 1, "S")
+        quantize_meas(0, 0)
+        quantize_us(0, 0)
+        quantize_meas(0, 1)
+        quantize_meas(0, 2)
+        group_us(0, 2, "V")
+        weights(0, 0)
+        quantize_us(0, 1)
+        quantize_us(0, 2)
+        for g in range(PD):
+            turn_meas(1, g, "S")
+        project(0, 0)
+        project(1, 0)
+        group_us(1, 0, "V")
+        group_us(1, 1, "S")
+        quantize_us(1, 0)
+        for g in range(PD):
+            quantize_meas(1, g)
+        weights(1, 0)
+        weights(0, 1)
+        project(2, 0)
+        project(3, 0)
+        group_us(1, 2, "V")
+        quantize_us(1, 1)
+        weigh(0, 0)
+        quantize_us(1, 2)
+        weights(1, 1)
+        project(0, 1)
+        weights(2, 0)
+        weigh(1, 0)
+        weigh(0, 1)
+        project(1, 1)
+        quantize_chunk(0)
+        weigh(2, 0)
+        weights(2, 1)
+        weigh(1, 1)
+        weights(3, 0)
+        side = [(("T", 2),), (("T", 3),), (("A", 0),), (), (("B", 0),), (("B", 1),), (("A", 1),), ()]
+        for c in range(8):
+            nxt = c + 2
+            if c == 4:
+                weights(c + 3, 0)
+            if 4 <= nxt < 8:
+                project(nxt, 0)
+            image_part(c, 0, "V")
+            if 4 <= nxt < 8:
+                weigh(nxt, 0)
+            if nxt == 3:
+                weigh(3, 0)
+            if c < 7:
+                quantize_chunk(c + 1)
+            image_part(c, 1, "S")
+            if nxt < 8:
+                project(nxt, 1)
+            if c < 5:
+                weights(c + 3, 1)
+            for kind, i in side[c]:
+                if kind == "T":
+                    for g in range(PD):
+                        turn_meas(i, g, "S")
+                if kind == "A":
+                    for j in range(PM):
+                        turn_group(i, j, 0, "V")
+                        turn_group(i, j, 1, "S")
+                if kind == "B":
+                    turn_basis(i, 0, "S")
+                    turn_basis(i, 1, "S")
+            if nxt < 8:
+                weigh(nxt, 1)
+            image_part(c, 2, "S")
+            if c < 3:
+                weights(c + 4, 0)
+            image_part(c, 3, "V" if c > 5 else "S")
+            for kind, i in side[c]:
+                if kind == "T":
+                    for g in range(PD):
+                        quantize_meas(i, g)
+                if kind == "A":
+                    for j in range(PM):
+                        quantize_group(i, j)
+                if kind == "B":
+                    quantize_basis(i)
+            if c == 3:
+                for r in range(4):
+                    widen_basis(r)
+        for r in range(4):
+            for j in range(PM):
+                comps_part(r, j, "VS"[j])

@@ -56,7 +56,7 @@ def tile_spectral_tikhonov_imaging_s8_kernel(
         sig = keep.tile([128, PM * 4], BF16, name="sig")
         nc.sync.dma_start(out=sig[:].rearrange("q (j t) -> q j t", j=PM), in_=sigma.rearrange("(j q t) -> q j t", j=PM, q=128))
         nc.sync.dma_start(out=lam_raw[0:64:32, :], in_=lam.partition_broadcast(2))
-        nc.sync.dma_start(out=d_rhs[64:66, :], in_=lam.partition_broadcast(2))
+        nc.sync.dma_start(out=lam_raw[64:66, :], in_=lam.partition_broadcast(2))
 
         raw_meas = []
         for pr in range(4):
@@ -92,9 +92,15 @@ def tile_spectral_tikhonov_imaging_s8_kernel(
 
         s2 = keep.tile([128, PM * 4], F32, name="s2")
         nc.vector.tensor_tensor(out=s2[:], in0=sig[:], in1=sig[:], op=MULT)
-        nc.vector.tensor_tensor(out=d_rhs[0:64, :], in0=lam_raw[0:64, :], in1=lam_raw[0:64, :], op=MULT)
+        by_chunk = "k (g p t) -> k g t p"
+        lam_v = lam_raw[:].rearrange(by_chunk, g=2, t=4)
+        d_rhs_v = d_rhs[:].rearrange("k (g t p) -> k g t p", g=2, t=4)
+        nc.vector.tensor_tensor(out=d_rhs_v[0:64], in0=lam_v[0:64], in1=lam_v[0:64], op=MULT)
+        nc.gpsimd.tensor_copy(out=d_rhs_v[64:66], in_=lam_v[64:66])
         lam_sq = keep.tile([128, F], F32, name="lam_sq")
-        nc.scalar.activation(out=lam_sq[0:64, :], in_=lam_raw[0:64, :], func=ACT.Square)
+        nc.scalar.activation(
+            out=lam_sq[:].rearrange("k (g t p) -> k g t p", g=2, t=4)[0:64], in_=lam_v[0:64], func=ACT.Square
+        )
         nc.vector.tensor_scalar(out=d_cols[:, :, 64], in0=s2[:], scalar1=2.0, scalar2=None, op0=MULT)
         s4 = keep.tile([128, PM * 4], F32, name="s4")
         nc.vector.tensor_tensor(out=s4[:], in0=s2[:], in1=s2[:], op=MULT)
@@ -122,7 +128,7 @@ def tile_spectral_tikhonov_imaging_s8_kernel(
                 nc.tensor.matmul(
                     out=bank[:, t, :],
                     lhsT=d_lhs[:, 4 * j + t, :],
-                    rhs=d_rhs[:, 512 * (c // 4) + c % 4 : 512 * (c // 4) + 512 : 4],
+                    rhs=d_rhs[:, 128 * c : 128 * c + 128],
                     start=True,
                     stop=True,
                 )

from contextlib import ExitStack

import concourse.mybir as mybir
from concourse.masks import make_identity

F, D, M, P, R = 1024, 1536, 1024, 2048, 512
FLOPS = 2 * (F * D * M + F * M * P + R * F * M)

F32 = mybir.dt.float32
BF16 = mybir.dt.bfloat16
U32 = mybir.dt.uint32
U8 = mybir.dt.uint8
I32 = mybir.dt.int32
E4M3 = mybir.dt.float8_e4m3fn
FP8X4 = mybir.dt.float8_e4m3fn_x4
FP4X4 = mybir.dt.float4_e2m1fn_x4
ACT = mybir.ActivationFunctionType
MULT = mybir.AluOpType.mult
SUB = mybir.AluOpType.subtract

PD = D // 512
PM = M // 512
PF = F // 512
AB, TP = 5, 3


def tile_spectral_tikhonov_imaging_s8_kernel(
    tc, meas, us, sigma, lam, vt_words, vt_scales, basis_bytes, basis_scale, image, comps
):
    nc = tc.nc
    with ExitStack() as ctx:
        keep = ctx.enter_context(tc.tile_pool(name="keep", bufs=1))
        work = ctx.enter_context(tc.tile_pool(name="work", bufs=2))
        stage = ctx.enter_context(tc.tile_pool(name="stage", bufs=6))
        psum = ctx.enter_context(tc.psum_pool(name="psum", bufs=1))

        ctx.enter_context(tc.manual_schedule())

        lam_raw = keep.tile([128, F], BF16, name="lam_raw")
        nc.vector.memset(lam_raw[0:64, :], 0.0)
        d_rhs = keep.tile([128, F], BF16, name="d_rhs")
        nc.gpsimd.memset(d_rhs[:], 1.0)
        d_cols = keep.tile([128, PM * 4, 128], BF16, name="d_cols")
        nc.vector.memset(d_cols[:], 0.0)
        nc.vector.memset(d_cols[:, :, 0:33:32], 1.0)
        warm = keep.tile([128, 1], F32, name="warm")
        nc.vector.memset(warm[:], 1.0)
        nc.scalar.activation(out=warm[:], in_=warm[:], func=ACT.Abs_reciprocal_sqrt)
        ident = keep.tile([128, 128], F32, name="ident")
        make_identity(nc, ident[:])
        ident_b = keep.tile([128, 128], BF16, name="ident_b")
        make_identity(nc, ident_b[:])
        vs = keep.tile([128, PM, P], U8, name="vs", align_bytes=64)
        nc.gpsimd.memset(vs[:].bitcast(I32), 0)

        sig = keep.tile([128, PM * 4], BF16, name="sig")
        nc.sync.dma_start(out=sig[:].rearrange("q (j t) -> q j t", j=PM), in_=sigma.rearrange("(j q t) -> q j t", j=PM, q=128))
        nc.sync.dma_start(out=lam_raw[0:64:32, :], in_=lam.partition_broadcast(2))
        nc.sync.dma_start(out=lam_raw[64:66, :], in_=lam.partition_broadcast(2))

        raw_meas = []
        for pr in range(4):
            raw_meas.append(keep.tile([128, 2, D], BF16, name="raw_meas%d" % pr))
        meas_v = meas.rearrange("(g p t) d -> g p t d", g=2, p=128)
        us_v = us.rearrange("(g p k) m -> g p k m", p=128, k=4)
        raw_us = {}

        def load_meas(pr):
            nc.sync.dma_start(out=raw_meas[pr][:], in_=meas_v[pr // 2, :, 2 * (pr % 2) : 2 * (pr % 2) + 2, :])

        load_meas(0)
        for j in range(PM):
            if j == 1:
                load_meas(1)
            for g in range(PD):
                t = stage.tile([128, 4, 512], BF16, name="raw_us", tag="stage", bufs=6)
                nc.sync.dma_start(out=t[:], in_=us_v[g, :, :, 512 * j : 512 * j + 512])
                raw_us[j, g] = t
        for q in range(4):
            nc.sync.dma_start(
                out=vs[32 * q : 32 * q + 4, :, :].bitcast(I32),
                in_=vt_scales[:, 4 * q : 4 * q + 4, :].rearrange("g r n -> r g n").bitcast(I32),
            )
        vt = keep.tile([128, PM, 2 * P], U8, name="vt", align_bytes=64)
        nc.sync.dma_start(out=vt[:], in_=vt_words.rearrange("g p n -> p g n"))
        for pr in range(2, 4):
            load_meas(pr)
        b_raw = keep.tile([128, 4, F], U8, name="b_raw")
        nc.sync.dma_start(out=b_raw[:], in_=basis_bytes.rearrange("(r p) f -> p r f", p=128))
        b_scale = keep.tile([128, F], F32, name="b_scale")
        nc.sync.dma_start(out=b_scale[:], in_=basis_scale.rearrange("o k -> (o k)").partition_broadcast(128))

        s2 = keep.tile([128, PM * 4], F32, name="s2")
        nc.vector.tensor_tensor(out=s2[:], in0=sig[:], in1=sig[:], op=MULT)
        by_chunk = "k (g p t) -> k g t p"
        lam_v = lam_raw[:].rearrange(by_chunk, g=2, t=4)
        d_rhs_v = d_rhs[:].rearrange("k (g t p) -> k g t p", g=2, t=4)
        nc.vector.tensor_tensor(out=d_rhs_v[0:64], in0=lam_v[0:64], in1=lam_v[0:64], op=MULT)
        nc.gpsimd.tensor_copy(out=d_rhs_v[64:66], in_=lam_v[64:66])
        lam_sq = keep.tile([128, F], F32, name="lam_sq")
        nc.scalar.activation(
            out=lam_sq[:].rearrange("k (g t p) -> k g t p", g=2, t=4)[0:64], in_=lam_v[0:64], func=ACT.Square
        )
        nc.vector.tensor_scalar(out=d_cols[:, :, 64], in0=s2[:], scalar1=2.0, scalar2=None, op0=MULT)
        s4 = keep.tile([128, PM * 4], F32, name="s4")
        nc.vector.tensor_tensor(out=s4[:], in0=s2[:], in1=s2[:], op=MULT)
        nc.vector.scalar_tensor_tensor(out=d_cols[:, :, 65], in0=s2[:], scalar=2.0, in1=d_cols[:, :, 64], op0=MULT, op1=SUB)
        nc.vector.tensor_copy(out=d_cols[:, :, 96], in_=s4[:])
        rest = keep.tile([128, PM * 4], F32, name="rest")
        nc.vector.tensor_tensor(out=rest[:], in0=s4[:], in1=d_cols[:, :, 96], op=SUB)
        nc.vector.tensor_copy(out=d_cols[:, :, 97], in_=rest[:])
        nc.vector.tensor_tensor(out=d_cols[:, :, 98], in0=rest[:], in1=d_cols[:, :, 97], op=SUB)
        nc.vector.tensor_tensor(out=d_rhs[32:64, :], in0=lam_sq[32:64, :], in1=d_rhs[32:64, :], op=SUB)
        d_lhs = keep.tile([128, PM * 4, 128], BF16, name="d_lhs")

        def square_lhs():
            d_turn = psum.tile([128, PM * 4, 128], BF16, name="d_turn", tag="acc", bufs=AB)
            for i in range(PM * 4):
                nc.tensor.transpose(d_turn[:, i, :], d_cols[:, i, :], ident_b[:])
            nc.vector.tensor_copy(out=d_lhs[:], in_=d_turn[:])

        copy_on = {"S": nc.scalar.copy, "V": nc.vector.tensor_copy}
        r2, tiles = {}, {}

        def weights(c, j):
            bank = psum.tile([128, 4, 128], F32, name="wb", tag="tp", bufs=TP)
            for t in range(4):
                nc.tensor.matmul(
                    out=bank[:, t, :],
                    lhsT=d_lhs[:, 4 * j + t, :],
                    rhs=d_rhs[:, 128 * c : 128 * c + 128],
                    start=True,
                    stop=True,
                )
            r2[c, j] = work.tile([128, 128, 4], F32, name="r2", bufs=16)
            nc.scalar.activation(out=r2[c, j][:], in_=bank[:].rearrange("q t f -> q f t"), func=ACT.Abs_reciprocal_sqrt)

        def turn_meas(pr, g, eng):
            if g == 0:
                tiles["mc", pr] = keep.tile([128, PD, 256], U32, name="mc%d" % pr, align_bytes=64)
                tiles["ms", pr] = keep.tile([128, PD, 256], U8, name="ms%d" % pr, align_bytes=64)
            words = raw_meas[pr][:].bitcast(F32)
            tp = psum.tile([128, 2, 2, 128], F32, name="tp", tag="tp", bufs=TP)
            for c in range(2):
                for u in range(2):
                    nc.tensor.transpose(tp[:, c, u, :], words[:, c, 256 * g + u : 256 * g + 256 : 2], ident[:])
            grouped = work.tile([128, 1024], BF16, name="mg", align_bytes=64, bufs=4)
            tiles["mg", pr, g] = grouped
            dst = grouped[:].bitcast(F32).rearrange("p (c r u) -> p c r u", c=2, u=2)
            copy_on[eng](out=dst, in_=tp[:].rearrange("p c u r -> p c r u"))

        def quantize_meas(pr, g):
            nc.vector.quantize_mx(
                out=tiles["mc", pr][:, g, :].bitcast(FP8X4), scales=tiles["ms", pr][:, g, :], in_=tiles["mg", pr, g][:]
            )

        uc = keep.tile([128, PD, M], U32, name="uc", align_bytes=64)
        usc = keep.tile([128, PD, M], U8, name="usc", align_bytes=64)

        def group_us(j, g, eng):
            grouped = work.tile([128, 4, 128, 4], BF16, name="ug", align_bytes=64, bufs=3)
            tiles["ug", j, g] = grouped
            copy_on[eng](out=grouped[:], in_=raw_us[j, g][:].rearrange("p k (q t) -> p t q k", t=4))

        def quantize_us(j, g):
            nc.vector.quantize_mx(
                out=uc[:, g, 512 * j : 512 * j + 512].bitcast(FP8X4),
                scales=usc[:, g, 512 * j : 512 * j + 512],
                in_=tiles["ug", j, g][:].rearrange("p t q k -> p (t q k)"),
            )

        hb, hc, hs = {}, {}, {}

        def project(c, j):
            bank = psum.tile([128, 4, 128], F32, name="cb", tag="acc", bufs=AB)
            pr, half = c // 2, c % 2
            mc, ms = tiles["mc", pr], tiles["ms", pr]
            for t in range(4):
                col = 512 * j + 128 * t
                for g in range(PD):
                    nc.tensor.matmul_mx(
                        out=bank[:, t, :],
                        lhsT=uc[:, g, col : col + 128].bitcast(FP8X4),
                        lhsT_scale=usc[:, g, col : col + 128],
                        rhs=mc[:, g, 128 * half : 128 * half + 128].bitcast(FP8X4),
                        rhs_scale=ms[:, g, 128 * half : 128 * half + 128],
                        start=(g == 0),
                        stop=(g == PD - 1),
                    )
            tiles["cb", c, j] = bank

        def weigh(c, j):
            if j == 0:
                hb[c] = work.tile([128, PM, 128, 4], BF16, name="hb", align_bytes=64, bufs=6)
            bank = tiles["cb", c, j]
            nc.vector.tensor_tensor(out=hb[c][:, j], in0=bank[:].rearrange("q t f -> q f t"), in1=r2[c, j][:], op=MULT)

        def quantize_chunk(c):
            hc[c] = work.tile([128, PM, 128], U32, name="hc", align_bytes=64, bufs=3)
            hs[c] = work.tile([128, PM, 128], U8, name="hs", align_bytes=64, bufs=3)
            nc.vector.quantize_mx(
                out=hc[c][:].rearrange("q j f -> q (j f)").bitcast(FP8X4),
                scales=hs[c][:].rearrange("q j f -> q (j f)"),
                in_=hb[c][:].rearrange("q j f t -> q (j f t)"),
            )

        image_v = image.rearrange("(g p t) n -> g t p n", g=2, p=128)

        def image_part(c, n, eng):
            if n % 2 == 0:
                tiles["ob"] = stage.tile([128, 1024], F32, name="ob", tag="stage", bufs=6)
            ob = tiles["ob"]
            bank = psum.tile([128, 512], F32, name="ib", tag="acc", bufs=AB)
            for j in range(PM):
                nc.tensor.matmul_mx(
                    out=bank[:],
                    lhsT=hc[c][:, j, :].bitcast(FP8X4),
                    lhsT_scale=hs[c][:, j, :],
                    rhs=vt[:, j, 1024 * n : 1024 * n + 1024].bitcast(FP4X4),
                    rhs_scale=vs[:, j, 512 * n : 512 * n + 512],
                    start=(j == 0),
                    stop=(j == PM - 1),
                )
            copy_on[eng](out=ob[:, 512 * (n % 2) : 512 * (n % 2) + 512], in_=bank[:])
            if n % 2 == 1:
                two = slice(512 * n - 512, 512 * n + 512)
                nc.sync.dma_start(out=image_v[c // 4, c % 4, :, two], in_=ob[:])

        bc = keep.tile([128, PF, R], U32, name="bc", align_bytes=64)
        bsc = keep.tile([128, PF, R], U8, name="bsc", align_bytes=64)

        def widen_basis(r):
            tiles["bw", r] = keep.tile([128, F], BF16, name="bw%d" % r)
            nc.vector.tensor_tensor(out=tiles["bw", r][:], in0=b_raw[:, r, :].bitcast(E4M3), in1=b_scale[:], op=MULT)

        def turn_basis(g, h, eng):
            if h == 0:
                tiles["bg", g] = work.tile([128, 2, 1024], BF16, name="bg", align_bytes=64)
            tp = psum.tile([128, 2, 2, 128], F32, name="tp", tag="tp", bufs=TP)
            for r in range(2):
                words = tiles["bw", 2 * h + r][:].bitcast(F32)
                for u in range(2):
                    nc.tensor.transpose(tp[:, r, u, :], words[:, 256 * g + u : 256 * g + 256 : 2], ident[:])
            dst = tiles["bg", g][:, h].bitcast(F32).rearrange("p (r n u) -> p r n u", r=2, u=2)
            copy_on[eng](out=dst, in_=tp[:].rearrange("p r u n -> p r n u"))

        def quantize_basis(g):
            nc.vector.quantize_mx(
                out=bc[:, g, :].bitcast(FP8X4), scales=bsc[:, g, :], in_=tiles["bg", g][:].rearrange("p h n -> p (h n)")
            )

        ac, asc = {}, {}

        def turn_group(g, j, u, eng):
            if u == 0:
                if j == 0:
                    ac[g] = keep.tile([128, PM, 512], U32, name="ac%d" % g, align_bytes=64)
                    asc[g] = keep.tile([128, PM, 512], U8, name="asc%d" % g, align_bytes=64)
                tiles["ha"] = work.tile([128, 2, 256, 4], BF16, name="ha", align_bytes=64)
            tp = psum.tile([128, 4, 128], F32, name="tp", tag="tp", bufs=TP)
            for t in range(4):
                words = hb[4 * g + t][:, j].rearrange("q f t -> q (f t)").bitcast(F32)
                nc.tensor.transpose(tp[:, t, :], words[:, u:256:2], ident[:])
            copy_on[eng](out=tiles["ha"][:, u], in_=tp[:].bitcast(BF16).rearrange("p t n -> p n t"))
            tiles["ha", g, j] = tiles["ha"]

        def quantize_group(g, j):
            nc.vector.quantize_mx(
                out=ac[g][:, j, :].bitcast(FP8X4), scales=asc[g][:, j, :], in_=tiles["ha", g, j][:].rearrange("p u n t -> p (u n t)")
            )

        def comps_part(r, j, eng):
            if j == 0:
                tiles["co"] = stage.tile([128, M], F32, name="co", tag="stage", bufs=6)
            co = tiles["co"]
            bank = psum.tile([128, 512], F32, name="ib", tag="acc", bufs=AB)
            for g in range(PF):
                nc.tensor.matmul_mx(
                    out=bank[:],
                    lhsT=bc[:, g, 128 * r : 128 * r + 128].bitcast(FP8X4),
                    lhsT_scale=bsc[:, g, 128 * r : 128 * r + 128],
                    rhs=ac[g][:, j, :].bitcast(FP8X4),
                    rhs_scale=asc[g][:, j, :],
                    start=(g == 0),
                    stop=(g == PF - 1),
                )
            cols = slice(512 * j, 512 * j + 512)
            copy_on[eng](
                out=co[:, cols].rearrange("p (q u e) -> p q u e", u=2, e=2), in_=bank[:].rearrange("p (u q e) -> p q u e", u=2, e=2)
            )
            nc.sync.dma_start(out=comps[128 * r : 128 * r + 128, cols], in_=co[:, cols])

        square_lhs()
        for g in range(PD):
            turn_meas(0, g, "S")
        group_us(0, 0, "V")
        group_us(0, 1, "S")
        quantize_meas(0, 0)
        quantize_us(0, 0)
        quantize_meas(0, 1)
        quantize_meas(0, 2)
        group_us(0, 2, "V")
        weights(0, 0)
        quantize_us(0, 1)
        quantize_us(0, 2)
        for g in range(PD):
            turn_meas(1, g, "S")
        project(0, 0)
        project(1, 0)
        group_us(1, 0, "V")
        group_us(1, 1, "S")
        quantize_us(1, 0)
        for g in range(PD):
            quantize_meas(1, g)
        weights(1, 0)
        weights(0, 1)
        project(2, 0)
        project(3, 0)
        group_us(1, 2, "V")
        quantize_us(1, 1)
        weigh(0, 0)
        quantize_us(1, 2)
        weights(1, 1)
        project(0, 1)
        weights(2, 0)
        weigh(1, 0)
        weigh(0, 1)
        project(1, 1)
        quantize_chunk(0)
        weigh(2, 0)
        weights(2, 1)
        weigh(1, 1)
        weights(3, 0)
        side = [(("T", 2),), (("T", 3),), (("A", 0),), (), (("B", 0),), (("B", 1),), (("A", 1),), ()]
        for c in range(8):
            nxt = c + 2
            if c == 4:
                weights(c + 3, 0)
            if 4 <= nxt < 8:
                project(nxt, 0)
            image_part(c, 0, "V")
            if 4 <= nxt < 8:
                weigh(nxt, 0)
            if nxt == 3:
                weigh(3, 0)
            if c < 7:
                quantize_chunk(c + 1)
            image_part(c, 1, "S")
            if nxt < 8:
                project(nxt, 1)
            if c < 5:
                weights(c + 3, 1)
            for kind, i in side[c]:
                if kind == "T":
                    for g in range(PD):
                        turn_meas(i, g, "S")
                if kind == "A":
                    for j in range(PM):
                        turn_group(i, j, 0, "V")
                        turn_group(i, j, 1, "S")
                if kind == "B":
                    turn_basis(i, 0, "S")
                    turn_basis(i, 1, "S")
            if nxt < 8:
                weigh(nxt, 1)
            image_part(c, 2, "S")
            if c < 3:
                weights(c + 4, 0)
            image_part(c, 3, "V" if c > 5 else "S")
            for kind, i in side[c]:
                if kind == "T":
                    for g in range(PD):
                        quantize_meas(i, g)
                if kind == "A":
                    for j in range(PM):
                        quantize_group(i, j)
                if kind == "B":
                    quantize_basis(i)
            if c == 3:
                for r in range(4):
                    widen_basis(r)
        for r in range(4):
            for j in range(PM):
                comps_part(r, j, "VS"[j])
